import numpy as np
import ml_dtypes


def mxq(x, axis, fmt="e4m3"):
    dtype, down = {"e4m3": (ml_dtypes.float8_e4m3fn, 7), "e5m2": (ml_dtypes.float8_e5m2, 14)}[fmt]
    v = np.moveaxis(np.asarray(x, np.float32).astype(ml_dtypes.bfloat16).astype(np.float64), axis, -1)
    blocks = v.reshape(v.shape[:-1] + (-1, 32))
    amax = np.abs(blocks).max(-1, keepdims=True)
    byte = np.maximum(np.where(amax > 0, np.frexp(amax)[1] - 1 + 127, 0) - down, 1)
    scale = np.exp2(byte - 127.0)
    codes = (blocks / scale).astype(np.float32).astype(dtype).astype(np.float64)
    return np.moveaxis((codes * scale).reshape(v.shape), -1, axis)


WIDE = False


def mx_kscale(k, group=512):
    if not WIDE:
        return np.ones(k)
    levels = np.array([18, -18])
    if group != 512:
        return np.exp2(np.random.permutation(np.resize(levels, k // group))).repeat(group)
    if k % 512:
        return np.exp2(np.random.permutation(np.resize(levels, k // 32))).repeat(32)
    a = np.empty((k // 512, 16))
    for p in range(k // 512):
        a[p, :8] = np.random.permutation(np.resize(levels, 8))
        for g in range(8):
            far = levels[np.abs(levels - a[p, g]) >= 10]
            a[p, g + 8] = far[np.random.randint(len(far))]
    return np.exp2(a.ravel()).repeat(32)


def f64(x):
    return np.asarray(x).astype(np.float64)


def softplus(v):
    return np.log(1.0 + np.exp(v))


def sigmoid(v):
    return 1.0 / (1.0 + np.exp(-v))


G, D, M, O, N = 4, 128, 128, 128, 512


def setup_inputs():
    n = np.random.standard_normal
    s_d = mx_kscale(D, 0)
    s_o = mx_kscale(O, 0)
    return {
        "x": (n((G, D, N)) * s_d[:, None]).astype(np.float32),
        "w1": (n((G, D, M)) / np.sqrt(D) / s_d[:, None]).astype(np.float32),
        "w2": (n((G, D, M)) / np.sqrt(D) / s_d[:, None]).astype(np.float32),
        "gn": (np.random.uniform(0.5, 2.0, (G, M, 1))).astype(np.float32),
        "wo": (n((G, O, M)) / np.sqrt(O) / s_o[:, None]).astype(np.float32),
        "dy": (n((G, O, N)) * s_o[:, None]).astype(np.float32),
        "old": (0.3 * n((G, M, N))).astype(np.float32),
    }


def reference(x, w1, w2, gn, wo, dy, old):
    w1q = mxq(f64(w1), 1, "e4m3")
    xq = mxq(f64(x), 1, "e4m3")
    z1 = w1q.transpose(0, 2, 1) @ xq
    w2q = mxq(f64(w2), 1, "e4m3")
    z2 = w2q.transpose(0, 2, 1) @ xq
    sp = softplus(z1) * softplus(z2)
    woq = mxq(f64(wo), 1, "e4m3")
    dyq = mxq(f64(dy), 1, "e4m3")
    c0 = woq.transpose(0, 2, 1) @ dyq
    dsp = c0 * sigmoid(z1 - z2) / (sp * f64(gn) + 1.0) * f64(gn)
    dz1 = c0 * np.log(sp * f64(gn) + 1.0) * sigmoid(z1 - z2) * (1.0 - sigmoid(z1 - z2)) + dsp * softplus(z2) * sigmoid(z1)
    y = dz1 + f64(old)
    return y

@@ -1,0 +1,182 @@
+from contextlib import ExitStack
+
+import concourse.mybir as mybir
+
+G, D, M, N = 4, 128, 128, 512
+FLOPS = 3 * 2 * G * D * M * N
+
+F32 = mybir.dt.float32
+BF16 = mybir.dt.bfloat16
+U32 = mybir.dt.uint32
+U8 = mybir.dt.uint8
+FP8X4 = mybir.dt.float8_e4m3fn_x4
+ACT = mybir.ActivationFunctionType
+ALU = mybir.AluOpType
+
+P = 128
+PACK = 4
+ROWS = D // PACK
+LN_FLOOR = 2.0 ** -44
+X_VECTOR_COLS = 320
+
+
+def tile_rows_bsoftprod_kernel(tc, x, w1, w2, gn, wo, dy, old, out):
+    nc = tc.nc
+
+    with ExitStack() as ctx:
+        sb = ctx.enter_context(tc.tile_pool(name="sb", bufs=1))
+        psum = ctx.enter_context(tc.psum_pool(name="psum", bufs=1))
+        ctx.enter_context(tc.manual_schedule())
+
+        def load_operand(src, name):
+            width = src.shape[2]
+            raw = sb.tile([P, PACK, width], F32, name=name + "_raw")
+            nc.sync.dma_start(out=raw[:], in_=src.rearrange("g (p j) w -> (g p) j w", j=PACK))
+            return raw
+
+        def packed_tile(raw, name):
+            return sb.tile([P, raw.shape[2], PACK], BF16, name=name + "_packed", align_bytes=64)
+
+        def interleave(copy, packed, raw, c0, c1):
+            copy(
+                out=packed[:, c0:c1, :].rearrange("p (c i) t -> p c t i", i=4),
+                in_=raw[:, :, c0:c1].rearrange("p t (c i) -> p c t i", i=4),
+            )
+
+        def quantize(packed, name):
+            width = packed.shape[1]
+            codes = sb.tile([P, width], U32, name=name + "_codes", align_bytes=64)
+            scales = sb.tile([P, width], U8, name=name + "_scales", align_bytes=64)
+            nc.vector.quantize_mx(
+                out=codes[:].bitcast(FP8X4),
+                scales=scales[:],
+                in_=packed[:].rearrange("p w t -> p (w t)"),
+            )
+            return codes, scales
+
+        def product(bank, weights, moving, g):
+            rows = slice(ROWS * g, ROWS * (g + 1))
+            nc.tensor.matmul_mx(
+                out=bank[:],
+                lhsT=weights[0][rows, :].bitcast(FP8X4),
+                lhsT_scale=weights[1][rows, :],
+                rhs=moving[0][rows, :].bitcast(FP8X4),
+                rhs_scale=moving[1][rows, :],
+                start=True,
+                stop=True,
+            )
+
+        def per_group(name):
+            return [sb.tile([P, N], F32, name="%s%d" % (name, g)) for g in range(G)]
+
+        x_raw = load_operand(x, "x")
+        w1_raw = load_operand(w1, "w1")
+        w2_raw = load_operand(w2, "w2")
+        dy_raw = load_operand(dy, "dy")
+        wo_raw = load_operand(wo, "wo")
+        gain = sb.tile([P, G], F32)
+        with nc.allow_non_contiguous_dma(reason="one gain for each partition and group"):
+            nc.sync.dma_start(out=gain[:], in_=gn.rearrange("g m o -> m (g o)"))
+        old_sb = sb.tile([P, G, N], F32)
+        nc.sync.dma_start(out=old_sb[:], in_=old.rearrange("g m n -> m g n"))
+
+        floor = sb.tile([P, 1], F32)
+        nc.vector.memset(floor[:], LN_FLOOR)
+        warm = sb.tile([P, 1], F32)
+        nc.scalar.activation(out=warm[:], in_=floor[:], func=ACT.Sigmoid)
+
+        x_packed = packed_tile(x_raw, "x")
+        w1_packed = packed_tile(w1_raw, "w1")
+        w2_packed = packed_tile(w2_raw, "w2")
+        interleave(nc.vector.tensor_copy, x_packed, x_raw, 0, X_VECTOR_COLS)
+        interleave(nc.scalar.copy, x_packed, x_raw, X_VECTOR_COLS, N)
+        interleave(nc.vector.tensor_copy, w1_packed, w1_raw, 0, M)
+        interleave(nc.scalar.copy, w2_packed, w2_raw, 0, M)
+        xq = quantize(x_packed, "x")
+        w1q = quantize(w1_packed, "w1")
+        w2q = quantize(w2_packed, "w2")
+
+        bank_a = [psum.tile([M, N], F32, name="bank_a%d" % g) for g in range(G)]
+        bank_b = [psum.tile([M, N], F32, name="bank_b%d" % g) for g in range(G)]
+        for g in range(G):
+            product(bank_a[g], w1q, xq, g)
+            product(bank_b[g], w2q, xq, g)
+
+        p1, p2, z2, diff = per_group("p1"), per_group("p2"), per_group("z2"), per_group("diff")
+        dy_packed = packed_tile(dy_raw, "dy")
+        wo_packed = packed_tile(wo_raw, "wo")
+        for g in range(G):
+            nc.scalar.activation(out=p2[g][:], in_=bank_b[g][:], func=ACT.Sigmoid, scale=-1.0)
+            nc.scalar.activation(out=p1[g][:], in_=bank_a[g][:], func=ACT.Sigmoid, scale=-1.0)
+            nc.vector.tensor_copy(out=z2[g][:], in_=bank_b[g][:])
+            if g > 0:
+                nc.vector.tensor_tensor(
+                    out=diff[g - 1][:], in0=bank_a[g - 1][:], in1=z2[g - 1][:], op=ALU.subtract
+                )
+        interleave(nc.vector.tensor_copy, dy_packed, dy_raw, 0, N)
+        nc.vector.tensor_tensor(
+            out=diff[G - 1][:], in0=bank_a[G - 1][:], in1=z2[G - 1][:], op=ALU.subtract
+        )
+        interleave(nc.vector.tensor_copy, wo_packed, wo_raw, 0, M)
+        dyq = quantize(dy_packed, "dy")
+        woq = quantize(wo_packed, "wo")
+
+        l1, l2, ns1, ns2 = per_group("l1"), per_group("l2"), per_group("ns1"), per_group("ns2")
+        sp, big_l, bb = per_group("sp"), per_group("big_l"), per_group("bb")
+        for g in range(G):
+            nc.scalar.activation(out=l1[g][:], in_=p1[g][:], func=ACT.Ln, bias=floor[:])
+            nc.scalar.activation(out=l2[g][:], in_=p2[g][:], func=ACT.Ln, bias=floor[:])
+        for g in range(G + 1):
+            if g < G:
+                nc.vector.scalar_tensor_tensor(
+                    out=ns1[g][:], in0=bank_a[g][:], scalar=-1.0, in1=l1[g][:], op0=ALU.mult, op1=ALU.min
+                )
+                nc.vector.scalar_tensor_tensor(
+                    out=ns2[g][:], in0=bank_b[g][:], scalar=-1.0, in1=l2[g][:], op0=ALU.mult, op1=ALU.min
+                )
+                product(bank_b[g], woq, dyq, g)
+            else:
+                nc.vector.scalar_tensor_tensor(
+                    out=bb[0][:], in0=p1[0][:], scalar=-1.0, in1=ns2[0][:], op0=ALU.add, op1=ALU.mult
+                )
+            if g > 0:
+                nc.vector.tensor_tensor(
+                    out=sp[g - 1][:], in0=ns1[g - 1][:], in1=ns2[g - 1][:], op=ALU.mult
+                )
+                nc.scalar.activation(
+                    out=big_l[g - 1][:], in_=sp[g - 1][:], func=ACT.Ln, scale=gain[:, g - 1 : g], bias=1.0
+                )
+        for g in range(1, G):
+            nc.vector.scalar_tensor_tensor(
+                out=bb[g][:], in0=p1[g][:], scalar=-1.0, in1=ns2[g][:], op0=ALU.add, op1=ALU.mult
+            )
+
+        th, rec = per_group("th"), per_group("rec")
+        for g in range(G):
+            nc.scalar.activation(out=rec[g][:], in_=big_l[g][:], func=ACT.Exp, scale=-1.0)
+            nc.scalar.activation(out=th[g][:], in_=diff[g][:], func=ACT.Tanh, scale=0.5)
+
+        aa, br, tt, uu, vv, res = [per_group(nm) for nm in ("aa", "br", "tt", "uu", "vv", "res")]
+        for pair in ((0, 1), (2, 3)):
+            for g in pair:
+                nc.vector.scalar_tensor_tensor(
+                    out=br[g][:], in0=bb[g][:], scalar=gain[:, g : g + 1], in1=rec[g][:], op0=ALU.mult, op1=ALU.mult
+                )
+                nc.vector.scalar_tensor_tensor(
+                    out=aa[g][:], in0=th[g][:], scalar=-1.0, in1=big_l[g][:], op0=ALU.add, op1=ALU.mult
+                )
+            for g in pair:
+                nc.vector.scalar_tensor_tensor(
+                    out=tt[g][:], in0=aa[g][:], scalar=-0.5, in1=br[g][:], op0=ALU.mult, op1=ALU.add
+                )
+            for g in pair:
+                nc.vector.scalar_tensor_tensor(
+                    out=uu[g][:], in0=th[g][:], scalar=1.0, in1=tt[g][:], op0=ALU.add, op1=ALU.mult
+                )
+            for g in pair:
+                nc.vector.scalar_tensor_tensor(
+                    out=vv[g][:], in0=bank_b[g][:], scalar=0.5, in1=uu[g][:], op0=ALU.mult, op1=ALU.mult
+                )
+            for g in pair:
+                nc.vector.tensor_tensor(out=res[g][:], in0=vv[g][:], in1=old_sb[:, g, :], op=ALU.add)
+                nc.sync.dma_start(out=out[g], in_=res[g][:])

@@ -100,53 +100,50 @@ def tile_rows_bsoftprod_kernel(tc, x, w1, w2, gn, wo, dy, old, out):
         bank_b = [psum.tile([M, N], F32, name="bank_b%d" % g) for g in range(G)]
         for g in range(G):
             product(bank_a[g], w1q, xq, g)
+        for g in range(G):
             product(bank_b[g], w2q, xq, g)
 
         p1, p2, z2, diff = per_group("p1"), per_group("p2"), per_group("z2"), per_group("diff")
         dy_packed = packed_tile(dy_raw, "dy")
         wo_packed = packed_tile(wo_raw, "wo")
+
+        def difference(g):
+            nc.vector.tensor_tensor(out=diff[g][:], in0=bank_a[g][:], in1=z2[g][:], op=ALU.subtract)
+
         for g in range(G):
-            nc.scalar.activation(out=p2[g][:], in_=bank_b[g][:], func=ACT.Sigmoid, scale=-1.0)
             nc.scalar.activation(out=p1[g][:], in_=bank_a[g][:], func=ACT.Sigmoid, scale=-1.0)
             nc.vector.tensor_copy(out=z2[g][:], in_=bank_b[g][:])
-            if g > 0:
-                nc.vector.tensor_tensor(
-                    out=diff[g - 1][:], in0=bank_a[g - 1][:], in1=z2[g - 1][:], op=ALU.subtract
-                )
+        for g in range(G):
+            nc.scalar.activation(out=p2[g][:], in_=bank_b[g][:], func=ACT.Sigmoid, scale=-1.0)
         interleave(nc.vector.tensor_copy, dy_packed, dy_raw, 0, N)
-        nc.vector.tensor_tensor(
-            out=diff[G - 1][:], in0=bank_a[G - 1][:], in1=z2[G - 1][:], op=ALU.subtract
-        )
         interleave(nc.vector.tensor_copy, wo_packed, wo_raw, 0, M)
         dyq = quantize(dy_packed, "dy")
         woq = quantize(wo_packed, "wo")
+        difference(0)
+        difference(1)
 
         l1, l2, ns1, ns2 = per_group("l1"), per_group("l2"), per_group("ns1"), per_group("ns2")
         sp, big_l, bb = per_group("sp"), per_group("big_l"), per_group("bb")
         for g in range(G):
             nc.scalar.activation(out=l1[g][:], in_=p1[g][:], func=ACT.Ln, bias=floor[:])
             nc.scalar.activation(out=l2[g][:], in_=p2[g][:], func=ACT.Ln, bias=floor[:])
-        for g in range(G + 1):
-            if g < G:
-                nc.vector.scalar_tensor_tensor(
-                    out=ns1[g][:], in0=bank_a[g][:], scalar=-1.0, in1=l1[g][:], op0=ALU.mult, op1=ALU.min
-                )
-                nc.vector.scalar_tensor_tensor(
-                    out=ns2[g][:], in0=bank_b[g][:], scalar=-1.0, in1=l2[g][:], op0=ALU.mult, op1=ALU.min
-                )
-                product(bank_b[g], woq, dyq, g)
-            else:
-                nc.vector.scalar_tensor_tensor(
-                    out=bb[0][:], in0=p1[0][:], scalar=-1.0, in1=ns2[0][:], op0=ALU.add, op1=ALU.mult
-                )
-            if g > 0:
-                nc.vector.tensor_tensor(
-                    out=sp[g - 1][:], in0=ns1[g - 1][:], in1=ns2[g - 1][:], op=ALU.mult
-                )
-                nc.scalar.activation(
-                    out=big_l[g - 1][:], in_=sp[g - 1][:], func=ACT.Ln, scale=gain[:, g - 1 : g], bias=1.0
-                )
-        for g in range(1, G):
+        for g in range(G):
+            nc.vector.scalar_tensor_tensor(
+                out=ns1[g][:], in0=bank_a[g][:], scalar=-1.0, in1=l1[g][:], op0=ALU.mult, op1=ALU.min
+            )
+            nc.vector.scalar_tensor_tensor(
+                out=ns2[g][:], in0=bank_b[g][:], scalar=-1.0, in1=l2[g][:], op0=ALU.mult, op1=ALU.min
+            )
+            product(bank_b[g], woq, dyq, g)
+            if g < G - 1:
+                nc.gpsimd.tensor_tensor(out=sp[g][:], in0=ns1[g][:], in1=ns2[g][:], op=ALU.mult)
+        difference(2)
+        nc.vector.tensor_tensor(out=sp[G - 1][:], in0=ns1[G - 1][:], in1=ns2[G - 1][:], op=ALU.mult)
+        difference(3)
+        for g in range(G):
+            nc.scalar.activation(
+                out=big_l[g][:], in_=sp[g][:], func=ACT.Ln, scale=gain[:, g : g + 1], bias=1.0
+            )
             nc.vector.scalar_tensor_tensor(
                 out=bb[g][:], in0=p1[g][:], scalar=-1.0, in1=ns2[g][:], op0=ALU.add, op1=ALU.mult
             )

@@ -17,7 +17,8 @@ P = 128
 PACK = 4
 ROWS = D // PACK
 LN_FLOOR = 2.0 ** -44
-X_VECTOR_COLS = 320
+HALF = N // 2
+N_PASS = 128
 
 
 def tile_rows_bsoftprod_kernel(tc, x, w1, w2, gn, wo, dy, old, out):
@@ -28,14 +29,17 @@ def tile_rows_bsoftprod_kernel(tc, x, w1, w2, gn, wo, dy, old, out):
         psum = ctx.enter_context(tc.psum_pool(name="psum", bufs=1))
         ctx.enter_context(tc.manual_schedule())
 
-        def load_operand(src, name):
-            width = src.shape[2]
-            raw = sb.tile([P, PACK, width], F32, name=name + "_raw")
-            nc.sync.dma_start(out=raw[:], in_=src.rearrange("g (p j) w -> (g p) j w", j=PACK))
+        def load_operand(src, name, c0, c1):
+            raw = sb.tile([P, PACK, c1 - c0], F32, name=name + "_raw")
+            rows = src.rearrange("g (p j) w -> (g p) j w", j=PACK)
+            nc.sync.dma_start(out=raw[:], in_=rows[:, :, c0:c1])
             return raw
 
         def packed_tile(raw, name):
             return sb.tile([P, raw.shape[2], PACK], BF16, name=name + "_packed", align_bytes=64)
+
+        def gpsimd_copy(out, in_):
+            nc.gpsimd.tensor_scalar(out=out, in0=in_, scalar1=1.0, scalar2=0.0, op0=ALU.mult, op1=ALU.add)
 
         def interleave(copy, packed, raw, c0, c1):
             copy(
@@ -54,26 +58,28 @@ def tile_rows_bsoftprod_kernel(tc, x, w1, w2, gn, wo, dy, old, out):
             )
             return codes, scales
 
-        def product(bank, weights, moving, g):
+        def product(bank, first_col, weights, moving, g):
             rows = slice(ROWS * g, ROWS * (g + 1))
-            nc.tensor.matmul_mx(
-                out=bank[:],
-                lhsT=weights[0][rows, :].bitcast(FP8X4),
-                lhsT_scale=weights[1][rows, :],
-                rhs=moving[0][rows, :].bitcast(FP8X4),
-                rhs_scale=moving[1][rows, :],
-                start=True,
-                stop=True,
-            )
+            for c in range(0, moving[0].shape[1], N_PASS):
+                nc.tensor.matmul_mx(
+                    out=bank[:, first_col + c : first_col + c + N_PASS],
+                    lhsT=weights[0][rows, :].bitcast(FP8X4),
+                    lhsT_scale=weights[1][rows, :],
+                    rhs=moving[0][rows, c : c + N_PASS].bitcast(FP8X4),
+                    rhs_scale=moving[1][rows, c : c + N_PASS],
+                    start=True,
+                    stop=True,
+                )
 
         def per_group(name):
             return [sb.tile([P, N], F32, name="%s%d" % (name, g)) for g in range(G)]
 
-        x_raw = load_operand(x, "x")
-        w1_raw = load_operand(w1, "w1")
-        w2_raw = load_operand(w2, "w2")
-        dy_raw = load_operand(dy, "dy")
-        wo_raw = load_operand(wo, "wo")
+        xa_raw = load_operand(x, "xa", 0, HALF)
+        w1_raw = load_operand(w1, "w1", 0, M)
+        w2_raw = load_operand(w2, "w2", 0, M)
+        xb_raw = load_operand(x, "xb", HALF, N)
+        wo_raw = load_operand(wo, "wo", 0, M)
+        dy_raw = load_operand(dy, "dy", 0, N)
         gain = sb.tile([P, G], F32)
         with nc.allow_non_contiguous_dma(reason="one gain for each partition and group"):
             nc.sync.dma_start(out=gain[:], in_=gn.rearrange("g m o -> m (g o)"))
@@ -85,42 +91,48 @@ def tile_rows_bsoftprod_kernel(tc, x, w1, w2, gn, wo, dy, old, out):
         warm = sb.tile([P, 1], F32)
         nc.scalar.activation(out=warm[:], in_=floor[:], func=ACT.Sigmoid)
 
-        x_packed = packed_tile(x_raw, "x")
+        xa_packed = packed_tile(xa_raw, "xa")
+        xb_packed = packed_tile(xb_raw, "xb")
         w1_packed = packed_tile(w1_raw, "w1")
         w2_packed = packed_tile(w2_raw, "w2")
-        interleave(nc.vector.tensor_copy, x_packed, x_raw, 0, X_VECTOR_COLS)
-        interleave(nc.scalar.copy, x_packed, x_raw, X_VECTOR_COLS, N)
+        dy_packed = packed_tile(dy_raw, "dy")
+        wo_packed = packed_tile(wo_raw, "wo")
+        interleave(nc.vector.tensor_copy, xa_packed, xa_raw, 0, HALF)
         interleave(nc.vector.tensor_copy, w1_packed, w1_raw, 0, M)
         interleave(nc.scalar.copy, w2_packed, w2_raw, 0, M)
-        xq = quantize(x_packed, "x")
+        xaq = quantize(xa_packed, "xa")
         w1q = quantize(w1_packed, "w1")
         w2q = quantize(w2_packed, "w2")
+        interleave(nc.vector.tensor_copy, xb_packed, xb_raw, 0, HALF)
+        interleave(nc.vector.tensor_copy, wo_packed, wo_raw, 0, M)
+        xbq = quantize(xb_packed, "xb")
+        woq = quantize(wo_packed, "wo")
 
         bank_a = [psum.tile([M, N], F32, name="bank_a%d" % g) for g in range(G)]
         bank_b = [psum.tile([M, N], F32, name="bank_b%d" % g) for g in range(G)]
-        for g in range(G):
-            product(bank_a[g], w1q, xq, g)
-        for g in range(G):
-            product(bank_b[g], w2q, xq, g)
-
         p1, p2, z2, diff = per_group("p1"), per_group("p2"), per_group("z2"), per_group("diff")
-        dy_packed = packed_tile(dy_raw, "dy")
-        wo_packed = packed_tile(wo_raw, "wo")
 
         def difference(g):
             nc.vector.tensor_tensor(out=diff[g][:], in0=bank_a[g][:], in1=z2[g][:], op=ALU.subtract)
 
-        for g in range(G):
-            nc.scalar.activation(out=p1[g][:], in_=bank_a[g][:], func=ACT.Sigmoid, scale=-1.0)
-            nc.vector.tensor_copy(out=z2[g][:], in_=bank_b[g][:])
-        for g in range(G):
-            nc.scalar.activation(out=p2[g][:], in_=bank_b[g][:], func=ACT.Sigmoid, scale=-1.0)
-        interleave(nc.vector.tensor_copy, dy_packed, dy_raw, 0, N)
-        interleave(nc.vector.tensor_copy, wo_packed, wo_raw, 0, M)
-        dyq = quantize(dy_packed, "dy")
-        woq = quantize(wo_packed, "wo")
-        difference(0)
-        difference(1)
+        for first_col, xq in ((0, xaq), (HALF, xbq)):
+            cols = slice(first_col, first_col + HALF)
+            for g in range(G):
+                product(bank_a[g], first_col, w1q, xq, g)
+            for g in range(G):
+                product(bank_b[g], first_col, w2q, xq, g)
+                if first_col > 0:
+                    nc.vector.tensor_copy(out=z2[g][:], in_=bank_b[g][:])
+            for g in range(G):
+                nc.scalar.activation(out=p1[g][:, cols], in_=bank_a[g][:, cols], func=ACT.Sigmoid, scale=-1.0)
+            for g in range(G):
+                nc.scalar.activation(out=p2[g][:, cols], in_=bank_b[g][:, cols], func=ACT.Sigmoid, scale=-1.0)
+        interleave(gpsimd_copy, dy_packed, dy_raw, 0, HALF)
+        gain2 = sb.tile([P, G], F32)
+        nc.gpsimd.tensor_scalar(out=gain2[:], in0=gain[:], scalar1=2.0, scalar2=0.0, op0=ALU.mult, op1=ALU.add)
+        for g in range(G - 1):
+            difference(g)
+        interleave(nc.vector.tensor_copy, dy_packed, dy_raw, HALF, N)
 
         l1, l2, ns1, ns2 = per_group("l1"), per_group("l2"), per_group("ns1"), per_group("ns2")
         sp, big_l, bb = per_group("sp"), per_group("big_l"), per_group("bb")
@@ -131,15 +143,16 @@ def tile_rows_bsoftprod_kernel(tc, x, w1, w2, gn, wo, dy, old, out):
             nc.vector.scalar_tensor_tensor(
                 out=ns1[g][:], in0=bank_a[g][:], scalar=-1.0, in1=l1[g][:], op0=ALU.mult, op1=ALU.min
             )
+            if g == 0:
+                dyq = quantize(dy_packed, "dy")
             nc.vector.scalar_tensor_tensor(
                 out=ns2[g][:], in0=bank_b[g][:], scalar=-1.0, in1=l2[g][:], op0=ALU.mult, op1=ALU.min
             )
-            product(bank_b[g], woq, dyq, g)
+            product(bank_b[g], 0, woq, dyq, g)
             if g < G - 1:
                 nc.gpsimd.tensor_tensor(out=sp[g][:], in0=ns1[g][:], in1=ns2[g][:], op=ALU.mult)
-        difference(2)
+        difference(G - 1)
         nc.vector.tensor_tensor(out=sp[G - 1][:], in0=ns1[G - 1][:], in1=ns2[G - 1][:], op=ALU.mult)
-        difference(3)
         for g in range(G):
             nc.scalar.activation(
                 out=big_l[g][:], in_=sp[g][:], func=ACT.Ln, scale=gain[:, g : g + 1], bias=1.0
@@ -153,27 +166,38 @@ def tile_rows_bsoftprod_kernel(tc, x, w1, w2, gn, wo, dy, old, out):
             nc.scalar.activation(out=rec[g][:], in_=big_l[g][:], func=ACT.Exp, scale=-1.0)
             nc.scalar.activation(out=th[g][:], in_=diff[g][:], func=ACT.Tanh, scale=0.5)
 
-        aa, br, tt, uu, vv, res = [per_group(nm) for nm in ("aa", "br", "tt", "uu", "vv", "res")]
+        aa, xx, tt, vv = [per_group(nm) for nm in ("aa", "xx", "tt", "vv")]
+        br = [l1[0], l1[1], big_l[1], l1[3]]
+
+        def log_term(g):
+            nc.vector.scalar_tensor_tensor(
+                out=aa[g][:], in0=th[g][:], scalar=-1.0, in1=big_l[g][:], op0=ALU.add, op1=ALU.mult
+            )
+
+        for g in (0, 1):
+            nc.vector.tensor_tensor(out=br[g][:], in0=bb[g][:], in1=rec[g][:], op=ALU.mult)
+            log_term(g)
+        for g in (2, 3):
+            nc.gpsimd.tensor_tensor(out=br[g][:], in0=bb[g][:], in1=rec[g][:], op=ALU.mult)
+        for g in range(G):
+            nc.vector.scalar_tensor_tensor(
+                out=xx[g][:], in0=th[g][:], scalar=1.0, in1=bank_b[g][:], op0=ALU.add, op1=ALU.mult
+            )
         for pair in ((0, 1), (2, 3)):
+            if pair[0] > 0:
+                for g in pair:
+                    log_term(g)
             for g in pair:
                 nc.vector.scalar_tensor_tensor(
-                    out=br[g][:], in0=bb[g][:], scalar=gain[:, g : g + 1], in1=rec[g][:], op0=ALU.mult, op1=ALU.mult
-                )
-                nc.vector.scalar_tensor_tensor(
-                    out=aa[g][:], in0=th[g][:], scalar=-1.0, in1=big_l[g][:], op0=ALU.add, op1=ALU.mult
-                )
-            for g in pair:
-                nc.vector.scalar_tensor_tensor(
-                    out=tt[g][:], in0=aa[g][:], scalar=-0.5, in1=br[g][:], op0=ALU.mult, op1=ALU.add
+                    out=tt[g][:], in0=br[g][:], scalar=gain2[:, g : g + 1], in1=aa[g][:], op0=ALU.mult, op1=ALU.subtract
                 )
             for g in pair:
                 nc.vector.scalar_tensor_tensor(
-                    out=uu[g][:], in0=th[g][:], scalar=1.0, in1=tt[g][:], op0=ALU.add, op1=ALU.mult
+                    out=vv[g][:], in0=tt[g][:], scalar=0.25, in1=xx[g][:], op0=ALU.mult, op1=ALU.mult
                 )
             for g in pair:
-                nc.vector.scalar_tensor_tensor(
-                    out=vv[g][:], in0=bank_b[g][:], scalar=0.5, in1=uu[g][:], op0=ALU.mult, op1=ALU.mult
-                )
-            for g in pair:
-                nc.vector.tensor_tensor(out=res[g][:], in0=vv[g][:], in1=old_sb[:, g, :], op=ALU.add)
-                nc.sync.dma_start(out=out[g], in_=res[g][:])
+                pieces = ((0, N),) if g < G - 1 else ((0, HALF), (HALF, N))
+                for c0, c1 in pieces:
+                    piece = sb.tile([P, c1 - c0], F32, name="res%d_%d" % (g, c0))
+                    nc.vector.tensor_tensor(out=piece[:], in0=vv[g][:, c0:c1], in1=old_sb[:, g, c0:c1], op=ALU.add)
+                    nc.sync.dma_start(out=out[g, :, c0:c1], in_=piece[:])

@@ -38,13 +38,16 @@ def tile_rows_bsoftprod_kernel(tc, x, w1, w2, gn, wo, dy, old, out):
         def packed_tile(raw, name):
             return sb.tile([P, raw.shape[2], PACK], BF16, name=name + "_packed", align_bytes=64)
 
-        def gpsimd_copy(out, in_):
-            nc.gpsimd.tensor_scalar(out=out, in0=in_, scalar1=1.0, scalar2=0.0, op0=ALU.mult, op1=ALU.add)
+        def interleave_on_gpsimd(packed, raw):
+            nc.gpsimd.tensor_scalar(
+                out=packed[:], in0=raw[:].rearrange("p t w -> p w t"),
+                scalar1=1.0, scalar2=0.0, op0=ALU.mult, op1=ALU.add,
+            )
 
-        def interleave(copy, packed, raw, c0, c1):
+        def interleave(copy, packed, raw):
             copy(
-                out=packed[:, c0:c1, :].rearrange("p (c i) t -> p c t i", i=4),
-                in_=raw[:, :, c0:c1].rearrange("p t (c i) -> p c t i", i=4),
+                out=packed.rearrange("p (c i) t -> p c t i", i=4),
+                in_=raw.rearrange("p t (c i) -> p c t i", i=4),
             )
 
         def quantize(packed, name):
@@ -78,8 +81,8 @@ def tile_rows_bsoftprod_kernel(tc, x, w1, w2, gn, wo, dy, old, out):
         w1_raw = load_operand(w1, "w1", 0, M)
         w2_raw = load_operand(w2, "w2", 0, M)
         xb_raw = load_operand(x, "xb", HALF, N)
-        wo_raw = load_operand(wo, "wo", 0, M)
         dy_raw = load_operand(dy, "dy", 0, N)
+        wo_raw = load_operand(wo, "wo", 0, M)
         gain = sb.tile([P, G], F32)
         with nc.allow_non_contiguous_dma(reason="one gain for each partition and group"):
             nc.sync.dma_start(out=gain[:], in_=gn.rearrange("g m o -> m (g o)"))
@@ -92,21 +95,16 @@ def tile_rows_bsoftprod_kernel(tc, x, w1, w2, gn, wo, dy, old, out):
         nc.scalar.activation(out=warm[:], in_=floor[:], func=ACT.Sigmoid)
 
         xa_packed = packed_tile(xa_raw, "xa")
-        xb_packed = packed_tile(xb_raw, "xb")
         w1_packed = packed_tile(w1_raw, "w1")
         w2_packed = packed_tile(w2_raw, "w2")
         dy_packed = packed_tile(dy_raw, "dy")
         wo_packed = packed_tile(wo_raw, "wo")
-        interleave(nc.vector.tensor_copy, xa_packed, xa_raw, 0, HALF)
-        interleave(nc.vector.tensor_copy, w1_packed, w1_raw, 0, M)
-        interleave(nc.scalar.copy, w2_packed, w2_raw, 0, M)
+        interleave(nc.vector.tensor_copy, xa_packed[:], xa_raw[:])
+        interleave(nc.vector.tensor_copy, w1_packed[:], w1_raw[:])
+        interleave(nc.scalar.copy, w2_packed[:], w2_raw[:])
         xaq = quantize(xa_packed, "xa")
         w1q = quantize(w1_packed, "w1")
         w2q = quantize(w2_packed, "w2")
-        interleave(nc.vector.tensor_copy, xb_packed, xb_raw, 0, HALF)
-        interleave(nc.vector.tensor_copy, wo_packed, wo_raw, 0, M)
-        xbq = quantize(xb_packed, "xb")
-        woq = quantize(wo_packed, "wo")
 
         bank_a = [psum.tile([M, N], F32, name="bank_a%d" % g) for g in range(G)]
         bank_b = [psum.tile([M, N], F32, name="bank_b%d" % g) for g in range(G)]
@@ -115,24 +113,41 @@ def tile_rows_bsoftprod_kernel(tc, x, w1, w2, gn, wo, dy, old, out):
         def difference(g):
             nc.vector.tensor_tensor(out=diff[g][:], in0=bank_a[g][:], in1=z2[g][:], op=ALU.subtract)
 
-        for first_col, xq in ((0, xaq), (HALF, xbq)):
-            cols = slice(first_col, first_col + HALF)
+        def sigmoids(dst, banks, cols):
             for g in range(G):
-                product(bank_a[g], first_col, w1q, xq, g)
-            for g in range(G):
-                product(bank_b[g], first_col, w2q, xq, g)
-                if first_col > 0:
-                    nc.vector.tensor_copy(out=z2[g][:], in_=bank_b[g][:])
-            for g in range(G):
-                nc.scalar.activation(out=p1[g][:, cols], in_=bank_a[g][:, cols], func=ACT.Sigmoid, scale=-1.0)
-            for g in range(G):
-                nc.scalar.activation(out=p2[g][:, cols], in_=bank_b[g][:, cols], func=ACT.Sigmoid, scale=-1.0)
-        interleave(gpsimd_copy, dy_packed, dy_raw, 0, HALF)
+                nc.scalar.activation(out=dst[g][:, cols], in_=banks[g][:, cols], func=ACT.Sigmoid, scale=-1.0)
+
+        first, second = slice(0, HALF), slice(HALF, N)
+        for g in range(G):
+            product(bank_a[g], 0, w1q, xaq, g)
+        for g in range(G):
+            product(bank_b[g], 0, w2q, xaq, g)
+        sigmoids(p1, bank_a, first)
+        sigmoids(p2, bank_b, first)
+
+        xb_packed = [sb.tile([P, N_PASS, PACK], BF16, name="xb_packed%d" % q, align_bytes=64) for q in range(2)]
+        for q in range(2):
+            interleave(nc.vector.tensor_copy, xb_packed[q][:], xb_raw[:, :, q * N_PASS : (q + 1) * N_PASS])
+        xbq = [quantize(xb_packed[q], "xb%d" % q) for q in range(2)]
+        for g in range(G):
+            nc.vector.tensor_copy(out=z2[g][:, first], in_=bank_b[g][:, first])
+        for g in range(G):
+            for q in range(2):
+                product(bank_a[g], HALF + q * N_PASS, w1q, xbq[q], g)
+        for g in range(G):
+            for q in range(2):
+                product(bank_b[g], HALF + q * N_PASS, w2q, xbq[q], g)
+            nc.vector.tensor_copy(out=z2[g][:, second], in_=bank_b[g][:, second])
+        sigmoids(p1, bank_a, second)
+        sigmoids(p2, bank_b, second)
+
+        interleave_on_gpsimd(dy_packed, dy_raw)
+        interleave_on_gpsimd(wo_packed, wo_raw)
         gain2 = sb.tile([P, G], F32)
         nc.gpsimd.tensor_scalar(out=gain2[:], in0=gain[:], scalar1=2.0, scalar2=0.0, op0=ALU.mult, op1=ALU.add)
         for g in range(G - 1):
             difference(g)
-        interleave(nc.vector.tensor_copy, dy_packed, dy_raw, HALF, N)
+        dyq = quantize(dy_packed, "dy")
 
         l1, l2, ns1, ns2 = per_group("l1"), per_group("l2"), per_group("ns1"), per_group("ns2")
         sp, big_l, bb = per_group("sp"), per_group("big_l"), per_group("bb")
@@ -144,7 +159,7 @@ def tile_rows_bsoftprod_kernel(tc, x, w1, w2, gn, wo, dy, old, out):
                 out=ns1[g][:], in0=bank_a[g][:], scalar=-1.0, in1=l1[g][:], op0=ALU.mult, op1=ALU.min
             )
             if g == 0:
-                dyq = quantize(dy_packed, "dy")
+                woq = quantize(wo_packed, "wo")
             nc.vector.scalar_tensor_tensor(
                 out=ns2[g][:], in0=bank_b[g][:], scalar=-1.0, in1=l2[g][:], op0=ALU.mult, op1=ALU.min
             )

@@ -16,39 +16,45 @@ ALU = mybir.AluOpType
 P = 128
 PACK = 4
 ROWS = D // PACK
-LN_FLOOR = 2.0 ** -44
-HALF = N // 2
 N_PASS = 128
+RUN = 4
+HALF = N // 2
+FLOOR_ARG = -30.0
+LAST = G - 1
 
 
 def tile_rows_bsoftprod_kernel(tc, x, w1, w2, gn, wo, dy, old, out):
     nc = tc.nc
+    first, second, whole = slice(0, HALF), slice(HALF, N), slice(0, N)
 
     with ExitStack() as ctx:
         sb = ctx.enter_context(tc.tile_pool(name="sb", bufs=1))
         psum = ctx.enter_context(tc.psum_pool(name="psum", bufs=1))
         ctx.enter_context(tc.manual_schedule())
 
-        def load_operand(src, name, c0, c1):
-            raw = sb.tile([P, PACK, c1 - c0], F32, name=name + "_raw")
-            rows = src.rearrange("g (p j) w -> (g p) j w", j=PACK)
-            nc.sync.dma_start(out=raw[:], in_=rows[:, :, c0:c1])
+        def load_operand(src, name, cols):
+            raw = sb.tile([P, PACK, cols.stop - cols.start], F32, name=name + "_raw")
+            nc.sync.dma_start(out=raw[:], in_=src.rearrange("g (p j) w -> (g p) j w", j=PACK)[:, :, cols])
             return raw
 
-        def packed_tile(raw, name):
-            return sb.tile([P, raw.shape[2], PACK], BF16, name=name + "_packed", align_bytes=64)
+        def packed_tile(width, name):
+            return sb.tile([P, width, PACK], BF16, name=name + "_packed", align_bytes=64)
 
-        def interleave_on_gpsimd(packed, raw):
+        def interleave(copy, raw, name):
+            packed = packed_tile(raw.shape[2], name)
+            copy(
+                out=packed[:].rearrange("p (c i) j -> p c j i", i=RUN),
+                in_=raw.rearrange("p j (c i) -> p c j i", i=RUN),
+            )
+            return packed
+
+        def interleave_on_gpsimd(raw, name):
+            packed = packed_tile(raw.shape[2], name)
             nc.gpsimd.tensor_scalar(
-                out=packed[:], in0=raw[:].rearrange("p t w -> p w t"),
+                out=packed[:], in0=raw.rearrange("p j w -> p w j"),
                 scalar1=1.0, scalar2=0.0, op0=ALU.mult, op1=ALU.add,
             )
-
-        def interleave(copy, packed, raw):
-            copy(
-                out=packed.rearrange("p (c i) t -> p c t i", i=4),
-                in_=raw.rearrange("p t (c i) -> p c t i", i=4),
-            )
+            return packed
 
         def quantize(packed, name):
             width = packed.shape[1]
@@ -57,7 +63,7 @@ def tile_rows_bsoftprod_kernel(tc, x, w1, w2, gn, wo, dy, old, out):
             nc.vector.quantize_mx(
                 out=codes[:].bitcast(FP8X4),
                 scales=scales[:],
-                in_=packed[:].rearrange("p w t -> p (w t)"),
+                in_=packed[:].rearrange("p w j -> p (w j)"),
             )
             return codes, scales
 
@@ -77,142 +83,162 @@ def tile_rows_bsoftprod_kernel(tc, x, w1, w2, gn, wo, dy, old, out):
         def per_group(name):
             return [sb.tile([P, N], F32, name="%s%d" % (name, g)) for g in range(G)]
 
-        xa_raw = load_operand(x, "xa", 0, HALF)
-        w1_raw = load_operand(w1, "w1", 0, M)
-        w2_raw = load_operand(w2, "w2", 0, M)
-        xb_raw = load_operand(x, "xb", HALF, N)
-        dy_raw = load_operand(dy, "dy", 0, N)
-        wo_raw = load_operand(wo, "wo", 0, M)
+        features = slice(0, M)
+        x_first_raw = load_operand(x, "x_first", first)
+        w1_raw = load_operand(w1, "w1", features)
+        w2_raw = load_operand(w2, "w2", features)
+        x_second_raw = load_operand(x, "x_second", second)
+        dy_raw = load_operand(dy, "dy", whole)
+        wo_raw = load_operand(wo, "wo", features)
         gain = sb.tile([P, G], F32)
         with nc.allow_non_contiguous_dma(reason="one gain for each partition and group"):
             nc.sync.dma_start(out=gain[:], in_=gn.rearrange("g m o -> m (g o)"))
         old_sb = sb.tile([P, G, N], F32)
         nc.sync.dma_start(out=old_sb[:], in_=old.rearrange("g m n -> m g n"))
 
+        floor_arg = sb.tile([P, 1], F32)
+        nc.vector.memset(floor_arg[:], FLOOR_ARG)
         floor = sb.tile([P, 1], F32)
-        nc.vector.memset(floor[:], LN_FLOOR)
-        warm = sb.tile([P, 1], F32)
-        nc.scalar.activation(out=warm[:], in_=floor[:], func=ACT.Sigmoid)
+        nc.scalar.activation(out=floor[:], in_=floor_arg[:], func=ACT.Sigmoid)
 
-        xa_packed = packed_tile(xa_raw, "xa")
-        w1_packed = packed_tile(w1_raw, "w1")
-        w2_packed = packed_tile(w2_raw, "w2")
-        dy_packed = packed_tile(dy_raw, "dy")
-        wo_packed = packed_tile(wo_raw, "wo")
-        interleave(nc.vector.tensor_copy, xa_packed[:], xa_raw[:])
-        interleave(nc.vector.tensor_copy, w1_packed[:], w1_raw[:])
-        interleave(nc.scalar.copy, w2_packed[:], w2_raw[:])
-        xaq = quantize(xa_packed, "xa")
-        w1q = quantize(w1_packed, "w1")
-        w2q = quantize(w2_packed, "w2")
+        x_first_packed = interleave(nc.vector.tensor_copy, x_first_raw[:], "x_first")
+        w1_packed = interleave(nc.vector.tensor_copy, w1_raw[:], "w1")
+        w2_packed = interleave(nc.scalar.copy, w2_raw[:], "w2")
+        x_first_q = quantize(x_first_packed, "x_first")
+        w1_q = quantize(w1_packed, "w1")
+        w2_q = quantize(w2_packed, "w2")
 
-        bank_a = [psum.tile([M, N], F32, name="bank_a%d" % g) for g in range(G)]
-        bank_b = [psum.tile([M, N], F32, name="bank_b%d" % g) for g in range(G)]
+        z1_bank = [psum.tile([M, N], F32, name="z1_bank%d" % g) for g in range(G)]
+        z2_c0_bank = [psum.tile([M, N], F32, name="z2_c0_bank%d" % g) for g in range(G)]
         p1, p2, z2, diff = per_group("p1"), per_group("p2"), per_group("z2"), per_group("diff")
-
-        def difference(g):
-            nc.vector.tensor_tensor(out=diff[g][:], in0=bank_a[g][:], in1=z2[g][:], op=ALU.subtract)
 
         def sigmoids(dst, banks, cols):
             for g in range(G):
                 nc.scalar.activation(out=dst[g][:, cols], in_=banks[g][:, cols], func=ACT.Sigmoid, scale=-1.0)
 
-        first, second = slice(0, HALF), slice(HALF, N)
-        for g in range(G):
-            product(bank_a[g], 0, w1q, xaq, g)
-        for g in range(G):
-            product(bank_b[g], 0, w2q, xaq, g)
-        sigmoids(p1, bank_a, first)
-        sigmoids(p2, bank_b, first)
+        def difference(g):
+            nc.vector.tensor_tensor(out=diff[g][:], in0=z1_bank[g][:], in1=z2[g][:], op=ALU.subtract)
 
-        xb_packed = [sb.tile([P, N_PASS, PACK], BF16, name="xb_packed%d" % q, align_bytes=64) for q in range(2)]
-        for q in range(2):
-            interleave(nc.vector.tensor_copy, xb_packed[q][:], xb_raw[:, :, q * N_PASS : (q + 1) * N_PASS])
-        xbq = [quantize(xb_packed[q], "xb%d" % q) for q in range(2)]
         for g in range(G):
-            nc.vector.tensor_copy(out=z2[g][:, first], in_=bank_b[g][:, first])
+            product(z1_bank[g], 0, w1_q, x_first_q, g)
         for g in range(G):
-            for q in range(2):
-                product(bank_a[g], HALF + q * N_PASS, w1q, xbq[q], g)
-        for g in range(G):
-            for q in range(2):
-                product(bank_b[g], HALF + q * N_PASS, w2q, xbq[q], g)
-            nc.vector.tensor_copy(out=z2[g][:, second], in_=bank_b[g][:, second])
-        sigmoids(p1, bank_a, second)
-        sigmoids(p2, bank_b, second)
+            product(z2_c0_bank[g], 0, w2_q, x_first_q, g)
+        sigmoids(p1, z1_bank, first)
+        sigmoids(p2, z2_c0_bank, first)
 
-        interleave_on_gpsimd(dy_packed, dy_raw)
-        interleave_on_gpsimd(wo_packed, wo_raw)
-        gain2 = sb.tile([P, G], F32)
-        nc.gpsimd.tensor_scalar(out=gain2[:], in0=gain[:], scalar1=2.0, scalar2=0.0, op0=ALU.mult, op1=ALU.add)
-        for g in range(G - 1):
+        starts = range(0, HALF, N_PASS)
+        x_second_packed = [
+            interleave(nc.vector.tensor_copy, x_second_raw[:, :, c : c + N_PASS], "x_second%d" % c) for c in starts
+        ]
+        x_second_q = [quantize(packed, "x_second%d" % c) for c, packed in zip(starts, x_second_packed)]
+        for g in range(G):
+            nc.vector.tensor_copy(out=z2[g][:, first], in_=z2_c0_bank[g][:, first])
+        for g in range(G):
+            for c, piece_q in zip(starts, x_second_q):
+                product(z1_bank[g], HALF + c, w1_q, piece_q, g)
+        for g in range(G):
+            for c, piece_q in zip(starts, x_second_q):
+                product(z2_c0_bank[g], HALF + c, w2_q, piece_q, g)
+            nc.vector.tensor_copy(out=z2[g][:, second], in_=z2_c0_bank[g][:, second])
+        sigmoids(p1, z1_bank, second)
+        sigmoids(p2, z2_c0_bank, second)
+
+        dy_packed = interleave_on_gpsimd(dy_raw[:], "dy")
+        wo_packed = interleave_on_gpsimd(wo_raw[:], "wo")
+        twice_gain = sb.tile([P, G], F32)
+        nc.gpsimd.tensor_scalar(out=twice_gain[:], in0=gain[:], scalar1=2.0, scalar2=0.0, op0=ALU.mult, op1=ALU.add)
+        for g in range(LAST):
             difference(g)
-        dyq = quantize(dy_packed, "dy")
+        dy_q = quantize(dy_packed, "dy")
 
-        l1, l2, ns1, ns2 = per_group("l1"), per_group("l2"), per_group("ns1"), per_group("ns2")
-        sp, big_l, bb = per_group("sp"), per_group("big_l"), per_group("bb")
+        ln_p1, ln_p2 = per_group("ln_p1"), per_group("ln_p2")
+        neg_sp1, neg_sp2 = per_group("neg_sp1"), per_group("neg_sp2")
+        sp, big_l, sig_sp = per_group("sp"), per_group("big_l"), per_group("sig_sp")
         for g in range(G):
-            nc.scalar.activation(out=l1[g][:], in_=p1[g][:], func=ACT.Ln, bias=floor[:])
-            nc.scalar.activation(out=l2[g][:], in_=p2[g][:], func=ACT.Ln, bias=floor[:])
-        for g in range(G):
+            nc.scalar.activation(out=ln_p1[g][:], in_=p1[g][:], func=ACT.Ln, bias=floor[:])
+            nc.scalar.activation(out=ln_p2[g][:], in_=p2[g][:], func=ACT.Ln, bias=floor[:])
+
+        def negated_softplus(dst, bank, ln_p):
             nc.vector.scalar_tensor_tensor(
-                out=ns1[g][:], in0=bank_a[g][:], scalar=-1.0, in1=l1[g][:], op0=ALU.mult, op1=ALU.min
+                out=dst[:], in0=bank[:], scalar=-1.0, in1=ln_p[:], op0=ALU.mult, op1=ALU.min
             )
+
+        for g in range(G):
+            negated_softplus(neg_sp1[g], z1_bank[g], ln_p1[g])
             if g == 0:
-                woq = quantize(wo_packed, "wo")
-            nc.vector.scalar_tensor_tensor(
-                out=ns2[g][:], in0=bank_b[g][:], scalar=-1.0, in1=l2[g][:], op0=ALU.mult, op1=ALU.min
+                wo_q = quantize(wo_packed, "wo")
+            negated_softplus(neg_sp2[g], z2_c0_bank[g], ln_p2[g])
+            product(z2_c0_bank[g], 0, wo_q, dy_q, g)
+            if g < LAST:
+                nc.gpsimd.tensor_tensor(out=sp[g][:], in0=neg_sp1[g][:], in1=neg_sp2[g][:], op=ALU.mult)
+        difference(LAST)
+        for cols in (first, second):
+            nc.vector.tensor_tensor(
+                out=sp[LAST][:, cols], in0=neg_sp1[LAST][:, cols], in1=neg_sp2[LAST][:, cols], op=ALU.mult
             )
-            product(bank_b[g], 0, woq, dyq, g)
-            if g < G - 1:
-                nc.gpsimd.tensor_tensor(out=sp[g][:], in0=ns1[g][:], in1=ns2[g][:], op=ALU.mult)
-        difference(G - 1)
-        nc.vector.tensor_tensor(out=sp[G - 1][:], in0=ns1[G - 1][:], in1=ns2[G - 1][:], op=ALU.mult)
         for g in range(G):
-            nc.scalar.activation(
-                out=big_l[g][:], in_=sp[g][:], func=ACT.Ln, scale=gain[:, g : g + 1], bias=1.0
-            )
+            for cols in (whole,) if g < LAST else (first, second):
+                nc.scalar.activation(
+                    out=big_l[g][:, cols], in_=sp[g][:, cols], func=ACT.Ln, scale=gain[:, g : g + 1], bias=1.0
+                )
             nc.vector.scalar_tensor_tensor(
-                out=bb[g][:], in0=p1[g][:], scalar=-1.0, in1=ns2[g][:], op0=ALU.add, op1=ALU.mult
+                out=sig_sp[g][:], in0=p1[g][:], scalar=-1.0, in1=neg_sp2[g][:], op0=ALU.add, op1=ALU.mult
             )
 
-        th, rec = per_group("th"), per_group("rec")
+        inverse, t = per_group("inverse"), per_group("t")
         for g in range(G):
-            nc.scalar.activation(out=rec[g][:], in_=big_l[g][:], func=ACT.Exp, scale=-1.0)
-            nc.scalar.activation(out=th[g][:], in_=diff[g][:], func=ACT.Tanh, scale=0.5)
+            nc.scalar.activation(out=inverse[g][:], in_=big_l[g][:], func=ACT.Exp, scale=-1.0)
+            nc.scalar.activation(out=t[g][:], in_=diff[g][:], func=ACT.Tanh, scale=0.5)
 
-        aa, xx, tt, vv = [per_group(nm) for nm in ("aa", "xx", "tt", "vv")]
-        br = [l1[0], l1[1], big_l[1], l1[3]]
+        log_term, gated_c0 = per_group("log_term"), per_group("gated_c0")
+        bracket, dz1 = per_group("bracket"), per_group("dz1")
+        ratio = [ln_p1[0], ln_p1[1], big_l[1], ln_p1[3]]
 
-        def log_term(g):
+        def make_log_term(g):
             nc.vector.scalar_tensor_tensor(
-                out=aa[g][:], in0=th[g][:], scalar=-1.0, in1=big_l[g][:], op0=ALU.add, op1=ALU.mult
+                out=log_term[g][:], in0=t[g][:], scalar=-1.0, in1=big_l[g][:], op0=ALU.add, op1=ALU.mult
             )
+
+        def make_bracket(g):
+            nc.vector.scalar_tensor_tensor(
+                out=bracket[g][:], in0=ratio[g][:], scalar=twice_gain[:, g : g + 1], in1=log_term[g][:],
+                op0=ALU.mult, op1=ALU.subtract,
+            )
+
+        def make_dz1(g, cols):
+            nc.vector.scalar_tensor_tensor(
+                out=dz1[g][:, cols], in0=bracket[g][:, cols], scalar=0.25, in1=gated_c0[g][:, cols],
+                op0=ALU.mult, op1=ALU.mult,
+            )
+
+        def add_old_and_store(g, cols):
+            result = sb.tile([P, cols.stop - cols.start], F32, name="result%d_%d" % (g, cols.start))
+            nc.vector.tensor_tensor(out=result[:], in0=dz1[g][:, cols], in1=old_sb[:, g, cols], op=ALU.add)
+            nc.sync.dma_start(out=out[g, :, cols], in_=result[:])
 
         for g in (0, 1):
-            nc.vector.tensor_tensor(out=br[g][:], in0=bb[g][:], in1=rec[g][:], op=ALU.mult)
-            log_term(g)
+            nc.vector.tensor_tensor(out=ratio[g][:], in0=sig_sp[g][:], in1=inverse[g][:], op=ALU.mult)
+            make_log_term(g)
         for g in (2, 3):
-            nc.gpsimd.tensor_tensor(out=br[g][:], in0=bb[g][:], in1=rec[g][:], op=ALU.mult)
+            nc.gpsimd.tensor_tensor(out=ratio[g][:], in0=sig_sp[g][:], in1=inverse[g][:], op=ALU.mult)
         for g in range(G):
             nc.vector.scalar_tensor_tensor(
-                out=xx[g][:], in0=th[g][:], scalar=1.0, in1=bank_b[g][:], op0=ALU.add, op1=ALU.mult
+                out=gated_c0[g][:], in0=t[g][:], scalar=1.0, in1=z2_c0_bank[g][:], op0=ALU.add, op1=ALU.mult
             )
-        for pair in ((0, 1), (2, 3)):
-            if pair[0] > 0:
-                for g in pair:
-                    log_term(g)
-            for g in pair:
-                nc.vector.scalar_tensor_tensor(
-                    out=tt[g][:], in0=br[g][:], scalar=gain2[:, g : g + 1], in1=aa[g][:], op0=ALU.mult, op1=ALU.subtract
-                )
-            for g in pair:
-                nc.vector.scalar_tensor_tensor(
-                    out=vv[g][:], in0=tt[g][:], scalar=0.25, in1=xx[g][:], op0=ALU.mult, op1=ALU.mult
-                )
-            for g in pair:
-                pieces = ((0, N),) if g < G - 1 else ((0, HALF), (HALF, N))
-                for c0, c1 in pieces:
-                    piece = sb.tile([P, c1 - c0], F32, name="res%d_%d" % (g, c0))
-                    nc.vector.tensor_tensor(out=piece[:], in0=vv[g][:, c0:c1], in1=old_sb[:, g, c0:c1], op=ALU.add)
-                    nc.sync.dma_start(out=out[g, :, c0:c1], in_=piece[:])
+
+        make_bracket(0)
+        make_bracket(1)
+        make_dz1(0, whole)
+        make_dz1(1, whole)
+        add_old_and_store(0, whole)
+        make_log_term(2)
+        add_old_and_store(1, whole)
+        make_bracket(2)
+        make_log_term(3)
+        make_dz1(2, whole)
+        make_bracket(3)
+        add_old_and_store(2, whole)
+        make_dz1(3, first)
+        make_dz1(3, second)
+        add_old_and_store(3, first)
+        add_old_and_store(3, second)

from contextlib import ExitStack

import concourse.mybir as mybir

G, D, M, N = 4, 128, 128, 512
FLOPS = 3 * 2 * G * D * M * N

F32 = mybir.dt.float32
BF16 = mybir.dt.bfloat16
U32 = mybir.dt.uint32
U8 = mybir.dt.uint8
FP8X4 = mybir.dt.float8_e4m3fn_x4
ACT = mybir.ActivationFunctionType
ALU = mybir.AluOpType

P = 128
PACK = 4
ROWS = D // PACK
N_PASS = 128
RUN = 4
HALF = N // 2
FLOOR_ARG = -30.0
LAST = G - 1


def tile_rows_bsoftprod_kernel(tc, x, w1, w2, gn, wo, dy, old, out):
    nc = tc.nc
    first, second, whole = slice(0, HALF), slice(HALF, N), slice(0, N)

    with ExitStack() as ctx:
        sb = ctx.enter_context(tc.tile_pool(name="sb", bufs=1))
        psum = ctx.enter_context(tc.psum_pool(name="psum", bufs=1))
        ctx.enter_context(tc.manual_schedule())

        def load_operand(src, name, cols):
            raw = sb.tile([P, PACK, cols.stop - cols.start], F32, name=name + "_raw")
            nc.sync.dma_start(out=raw[:], in_=src.rearrange("g (p j) w -> (g p) j w", j=PACK)[:, :, cols])
            return raw

        def packed_tile(width, name):
            return sb.tile([P, width, PACK], BF16, name=name + "_packed", align_bytes=64)

        def interleave(copy, raw, name):
            packed = packed_tile(raw.shape[2], name)
            copy(
                out=packed[:].rearrange("p (c i) j -> p c j i", i=RUN),
                in_=raw.rearrange("p j (c i) -> p c j i", i=RUN),
            )
            return packed

        def interleave_on_gpsimd(raw, name):
            packed = packed_tile(raw.shape[2], name)
            nc.gpsimd.tensor_scalar(
                out=packed[:], in0=raw.rearrange("p j w -> p w j"),
                scalar1=1.0, scalar2=0.0, op0=ALU.mult, op1=ALU.add,
            )
            return packed

        def quantize(packed, name):
            width = packed.shape[1]
            codes = sb.tile([P, width], U32, name=name + "_codes", align_bytes=64)
            scales = sb.tile([P, width], U8, name=name + "_scales", align_bytes=64)
            nc.vector.quantize_mx(
                out=codes[:].bitcast(FP8X4),
                scales=scales[:],
                in_=packed[:].rearrange("p w j -> p (w j)"),
            )
            return codes, scales

        def product(bank, first_col, weights, moving, g):
            rows = slice(ROWS * g, ROWS * (g + 1))
            for c in range(0, moving[0].shape[1], N_PASS):
                nc.tensor.matmul_mx(
                    out=bank[:, first_col + c : first_col + c + N_PASS],
                    lhsT=weights[0][rows, :].bitcast(FP8X4),
                    lhsT_scale=weights[1][rows, :],
                    rhs=moving[0][rows, c : c + N_PASS].bitcast(FP8X4),
                    rhs_scale=moving[1][rows, c : c + N_PASS],
                    start=True,
                    stop=True,
                )

        def per_group(name):
            return [sb.tile([P, N], F32, name="%s%d" % (name, g)) for g in range(G)]

        features = slice(0, M)
        x_first_raw = load_operand(x, "x_first", first)
        w1_raw = load_operand(w1, "w1", features)
        w2_raw = load_operand(w2, "w2", features)
        x_second_raw = load_operand(x, "x_second", second)
        dy_raw = load_operand(dy, "dy", whole)
        wo_raw = load_operand(wo, "wo", features)
        gain = sb.tile([P, G], F32)
        with nc.allow_non_contiguous_dma(reason="one gain for each partition and group"):
            nc.sync.dma_start(out=gain[:], in_=gn.rearrange("g m o -> m (g o)"))
        old_sb = sb.tile([P, G, N], F32)
        nc.sync.dma_start(out=old_sb[:], in_=old.rearrange("g m n -> m g n"))

        floor_arg = sb.tile([P, 1], F32)
        nc.vector.memset(floor_arg[:], FLOOR_ARG)
        floor = sb.tile([P, 1], F32)
        nc.scalar.activation(out=floor[:], in_=floor_arg[:], func=ACT.Sigmoid)

        x_first_packed = interleave(nc.vector.tensor_copy, x_first_raw[:], "x_first")
        w1_packed = interleave(nc.vector.tensor_copy, w1_raw[:], "w1")
        w2_packed = interleave(nc.scalar.copy, w2_raw[:], "w2")
        x_first_q = quantize(x_first_packed, "x_first")
        w1_q = quantize(w1_packed, "w1")
        w2_q = quantize(w2_packed, "w2")

        z1_bank = [psum.tile([M, N], F32, name="z1_bank%d" % g) for g in range(G)]
        z2_c0_bank = [psum.tile([M, N], F32, name="z2_c0_bank%d" % g) for g in range(G)]
        p1, p2, z2, diff = per_group("p1"), per_group("p2"), per_group("z2"), per_group("diff")

        def sigmoids(dst, banks, cols):
            for g in range(G):
                nc.scalar.activation(out=dst[g][:, cols], in_=banks[g][:, cols], func=ACT.Sigmoid, scale=-1.0)

        def difference(g):
            nc.vector.tensor_tensor(out=diff[g][:], in0=z1_bank[g][:], in1=z2[g][:], op=ALU.subtract)

        for g in range(G):
            product(z1_bank[g], 0, w1_q, x_first_q, g)
        for g in range(G):
            product(z2_c0_bank[g], 0, w2_q, x_first_q, g)
        sigmoids(p1, z1_bank, first)
        sigmoids(p2, z2_c0_bank, first)

        starts = range(0, HALF, N_PASS)
        x_second_packed = [
            interleave(nc.vector.tensor_copy, x_second_raw[:, :, c : c + N_PASS], "x_second%d" % c) for c in starts
        ]
        x_second_q = [quantize(packed, "x_second%d" % c) for c, packed in zip(starts, x_second_packed)]
        for g in range(G):
            nc.vector.tensor_copy(out=z2[g][:, first], in_=z2_c0_bank[g][:, first])
        for g in range(G):
            for c, piece_q in zip(starts, x_second_q):
                product(z1_bank[g], HALF + c, w1_q, piece_q, g)
        for g in range(G):
            for c, piece_q in zip(starts, x_second_q):
                product(z2_c0_bank[g], HALF + c, w2_q, piece_q, g)
            nc.vector.tensor_copy(out=z2[g][:, second], in_=z2_c0_bank[g][:, second])
        sigmoids(p1, z1_bank, second)
        sigmoids(p2, z2_c0_bank, second)

        dy_packed = interleave_on_gpsimd(dy_raw[:], "dy")
        wo_packed = interleave_on_gpsimd(wo_raw[:], "wo")
        twice_gain = sb.tile([P, G], F32)
        nc.gpsimd.tensor_scalar(out=twice_gain[:], in0=gain[:], scalar1=2.0, scalar2=0.0, op0=ALU.mult, op1=ALU.add)
        for g in range(LAST):
            difference(g)
        dy_q = quantize(dy_packed, "dy")

        ln_p1, ln_p2 = per_group("ln_p1"), per_group("ln_p2")
        neg_sp1, neg_sp2 = per_group("neg_sp1"), per_group("neg_sp2")
        sp, big_l, sig_sp = per_group("sp"), per_group("big_l"), per_group("sig_sp")
        for g in range(G):
            nc.scalar.activation(out=ln_p1[g][:], in_=p1[g][:], func=ACT.Ln, bias=floor[:])
            nc.scalar.activation(out=ln_p2[g][:], in_=p2[g][:], func=ACT.Ln, bias=floor[:])

        def negated_softplus(dst, bank, ln_p):
            nc.vector.scalar_tensor_tensor(
                out=dst[:], in0=bank[:], scalar=-1.0, in1=ln_p[:], op0=ALU.mult, op1=ALU.min
            )

        for g in range(G):
            negated_softplus(neg_sp1[g], z1_bank[g], ln_p1[g])
            if g == 0:
                wo_q = quantize(wo_packed, "wo")
            negated_softplus(neg_sp2[g], z2_c0_bank[g], ln_p2[g])
            product(z2_c0_bank[g], 0, wo_q, dy_q, g)
            if g < LAST:
                nc.gpsimd.tensor_tensor(out=sp[g][:], in0=neg_sp1[g][:], in1=neg_sp2[g][:], op=ALU.mult)
        difference(LAST)
        for cols in (first, second):
            nc.vector.tensor_tensor(
                out=sp[LAST][:, cols], in0=neg_sp1[LAST][:, cols], in1=neg_sp2[LAST][:, cols], op=ALU.mult
            )
        for g in range(G):
            for cols in (whole,) if g < LAST else (first, second):
                nc.scalar.activation(
                    out=big_l[g][:, cols], in_=sp[g][:, cols], func=ACT.Ln, scale=gain[:, g : g + 1], bias=1.0
                )
            nc.vector.scalar_tensor_tensor(
                out=sig_sp[g][:], in0=p1[g][:], scalar=-1.0, in1=neg_sp2[g][:], op0=ALU.add, op1=ALU.mult
            )

        inverse, t = per_group("inverse"), per_group("t")
        for g in range(G):
            nc.scalar.activation(out=inverse[g][:], in_=big_l[g][:], func=ACT.Exp, scale=-1.0)
            nc.scalar.activation(out=t[g][:], in_=diff[g][:], func=ACT.Tanh, scale=0.5)

        log_term, gated_c0 = per_group("log_term"), per_group("gated_c0")
        bracket, dz1 = per_group("bracket"), per_group("dz1")
        ratio = [ln_p1[0], ln_p1[1], big_l[1], ln_p1[3]]

        def make_log_term(g):
            nc.vector.scalar_tensor_tensor(
                out=log_term[g][:], in0=t[g][:], scalar=-1.0, in1=big_l[g][:], op0=ALU.add, op1=ALU.mult
            )

        def make_bracket(g):
            nc.vector.scalar_tensor_tensor(
                out=bracket[g][:], in0=ratio[g][:], scalar=twice_gain[:, g : g + 1], in1=log_term[g][:],
                op0=ALU.mult, op1=ALU.subtract,
            )

        def make_dz1(g, cols):
            nc.vector.scalar_tensor_tensor(
                out=dz1[g][:, cols], in0=bracket[g][:, cols], scalar=0.25, in1=gated_c0[g][:, cols],
                op0=ALU.mult, op1=ALU.mult,
            )

        def add_old_and_store(g, cols):
            result = sb.tile([P, cols.stop - cols.start], F32, name="result%d_%d" % (g, cols.start))
            nc.vector.tensor_tensor(out=result[:], in0=dz1[g][:, cols], in1=old_sb[:, g, cols], op=ALU.add)
            nc.sync.dma_start(out=out[g, :, cols], in_=result[:])

        for g in (0, 1):
            nc.vector.tensor_tensor(out=ratio[g][:], in0=sig_sp[g][:], in1=inverse[g][:], op=ALU.mult)
            make_log_term(g)
        for g in (2, 3):
            nc.gpsimd.tensor_tensor(out=ratio[g][:], in0=sig_sp[g][:], in1=inverse[g][:], op=ALU.mult)
        for g in range(G):
            nc.vector.scalar_tensor_tensor(
                out=gated_c0[g][:], in0=t[g][:], scalar=1.0, in1=z2_c0_bank[g][:], op0=ALU.add, op1=ALU.mult
            )

        make_bracket(0)
        make_bracket(1)
        make_dz1(0, whole)
        make_dz1(1, whole)
        add_old_and_store(0, whole)
        make_log_term(2)
        add_old_and_store(1, whole)
        make_bracket(2)
        make_log_term(3)
        make_dz1(2, whole)
        make_bracket(3)
        add_old_and_store(2, whole)
        make_dz1(3, first)
        make_dz1(3, second)
        add_old_and_store(3, first)
        add_old_and_store(3, second)
